import numpy as np, ml_dtypes
CORES = [51,54,179,182]
N = 4
BF = ml_dtypes.bfloat16
def gentries(a):
    return np.ascontiguousarray(a.reshape(8, 16, -1).transpose(0, 2, 1)).reshape(8, -1)
def gtable(e):
    e = np.asarray(e); return np.ascontiguousarray(e.reshape(8, -1, 16).transpose(0, 2, 1)).reshape(128, -1).astype(np.int32)
G, C, K, RO, SH = 512, 2048, 256, 5, 9
NONE = N * G
def batch(rng, keep=(), high=()):
    key = rng.random((8, C)) * np.where(np.arange(C) >> SH == 0, 3.0, 1.0)
    for c in keep: key[:, c] += 4
    for g in high: key[g, :1 << SH] += 4
    s = np.ascontiguousarray(np.argsort(key, axis=1)[:, :N * K]); w = rng.integers(0, NONE, (8, 16, 4)); ro = np.zeros((8, 16, N * K), np.int64)
    for r in range(N):
        for t in range(16):
            if t < RO: ro[:, t, r * K:(r + 1) * K] = (r + t) % N * G + np.argsort(rng.random((8, G)), axis=1)[:, :K]
            else: ro[:, t, r * K:(r + 1) * K] = np.take_along_axis(w[:, t], rng.integers(0, 4, (8, K)), 1)
    return s, ro, w
def living(rng, s, ro, w, share):
    pa = np.full((8, 16, C), NONE, np.int64); live, dead = [], []
    for g in range(8):
        rest = rng.permutation(np.setdiff1d(np.arange(C), s[g])); h = max(int(len(rest) * share), 8)
        a = rest[h:]; m = len(a); v = rng.integers(0, NONE, (16, m))
        for k in range(RO, 16): v[k] = w[g, k][rng.integers(0, 4, m)]
        v = np.where(rng.random((16, m)) < 0.8 * rng.random((1, m)), ro[g][:, np.arange(m) % (N * K)], v)
        no = rng.random((16, m)) < 0.9 * rng.random((1, m)); no[rng.integers(0, 16, m), np.arange(m)] = False
        pa[g][:, a] = np.where(no, NONE, v); live.append(a); dead.append(rest[:h])
    return pa, live, dead
def trunks(rng, s, ro, live, dead):
    op = rng.integers(0, N * K, (N, 8, G))
    for t in rng.permutation(RO):
        for q in range(N):
            r = int((q - t) % N); np.put_along_axis(op[q], ro[:, t, r * K:(r + 1) * K] - q * G, np.ascontiguousarray(np.broadcast_to(r * K + np.arange(K), (8, K))), 1)
    tr = np.zeros((N, 8, 16, G), np.int64); sh = (N, 16, G)
    for g in range(8):
        a = live[g]; m = len(a); top = np.sort(a)[-(m >> 3):]; x = a[rng.integers(0, m, sh)]
        x = np.where(rng.random(sh) < rng.choice(np.array([0.3, 0.6, 0.8, 0.9, 1.0]), (N, 1, G)), top[rng.integers(0, len(top), sh)], x)
        x = np.where(rng.random(sh) < rng.choice(np.array([0.0, 0.1, 0.25]), (N, 1, G)), a[(op[:, g][:, None, :] + N * K * rng.integers(0, 2, sh)) % m], x)
        gone = np.concatenate([dead[g], s[g][::4]])
        tr[:, g] = np.where(rng.random(sh) < rng.choice(np.array([0.0, 0.0, 0.1, 0.3]), (N, 1, G)), gone[rng.integers(0, len(gone), sh)], x)
    return tr
def pack(tr, pa, s, ro):
    return {"trunk": np.ascontiguousarray(tr.reshape(N, 128, G)).astype(np.int32), "paths": np.stack([pa.reshape(128, C)] * N).astype(np.int32),
            "calls": np.stack([gtable(s[:, r * K:(r + 1) * K]) for r in range(N)]), "routes": np.stack([ro[:, :, r * K:(r + 1) * K].reshape(128, K) for r in range(N)]).astype(np.int32)}
def setup_inputs(rng):
    s, ro, w = batch(rng); pa, live, dead = living(rng, s, ro, w, 0.05)
    return pack(trunks(rng, s, ro, live, dead), pa, s, ro)
def setup_inputs_ties(rng):
    edge = np.array([0, C - 1] + [e for b in range(1, C >> SH) for e in ((b << SH) - 1, b << SH)])
    s, ro, w = batch(rng, edge); pa, live, dead = living(rng, s, ro, w, 0.05); tr = trunks(rng, s, ro, live, dead); sh = (N, 16, G); k = np.arange(16)[None, :, None]
    for g in range(8):
        a = np.union1d(live[g], edge); d = np.setdiff1d(np.append(dead[g], s[g][0]), edge)
        few = pa[g][:, live[g][:3]]; pa[g][:, a] = few[:, rng.integers(0, 3, len(a))]
        x = tr[:, g].copy(); x[:, 8:] = x[:, :8][:, ::-1].copy()
        kind = rng.integers(0, 5, (N, 1, G)); end = rng.choice(np.array([0, 15]), (N, 1, G)); z = a[rng.integers(0, len(a), sh)]
        x = np.where(kind == 1, edge[rng.integers(0, len(edge), sh)], np.where(kind == 2, z, x))
        tr[:, g] = np.where(kind == 3, np.where(k == end, d[rng.integers(0, len(d), sh)], z), x)
        j = rng.permutation(N * K)[:64]; r = j // K; c = rng.permutation(live[g])[:64]
        pa[g][:, c] = ro[g][:, j]; tr[r, g, rng.integers(0, 16, 64), ro[g, 0, j] - r * G] = c
        u = rng.permutation(np.setdiff1d(np.nonzero(s[g] >> SH == (C - 1) >> SH)[0], j))[:16]; q = u // K; at = ro[g, 0, u] - q * G
        b = np.sort(rng.permutation(np.setdiff1d(live[g][live[g] >> SH == 0], np.append(edge, c)))[:32].reshape(2, 16), axis=0)
        pa[g][:, b[0]] = ro[g][:, u]; pa[g][:, b[1]] = ro[g][:, u]; h = rng.integers(0, 16, 16)
        pa[g, h, b[0]] = np.where(rng.random(16) < 0.5, NONE, (ro[g, h, u] + 1) % NONE)
        y = tr[:, g]; e = rng.integers(0, 16, 16)
        y[q, :, at] = b[rng.integers(0, 2, (16, 16)), np.arange(16)[:, None]]
        y[q, e, at] = b[1]; y[q, (e + 8) & 15, at] = b[0]
    return pack(tr, pa, s, ro)
def setup_inputs_same(rng):
    few = np.array([0, 1, 2, (1 << SH) - 1]); keep = np.append(few, C - 1)
    s, ro, w = batch(rng, keep, (5, 6, 7)); pa, live, dead = living(rng, s, ro, w, 0.05); tr = trunks(rng, s, ro, live, dead); sh = (N, 16, G)
    for g in range(8):
        pa[g][:, keep] = ro[g][:, rng.integers(0, N * K, len(keep))]
        top = np.union1d(live[g][live[g] >> SH == (C - 1) >> SH], np.array([C - 1])); x = top[rng.integers(0, len(top), sh)]
        if g > 4:
            low = rng.permutation(live[g][live[g] >> SH == 0]); n = rng.permutation(N * K); q = np.arange(N * K) // K; at = ro[g, 0] - q * G
            if g == 5: i = (n >= 256).astype(np.int64) + (n >= 768)
            elif g == 6: i = (n >= 1024).astype(np.int64)
            else: i = np.arange(N * K) % len(low)
            y = np.where(tr[:, g] >> SH == 0, x, tr[:, g]); y[q, :, at] = x[q, :, at]
            y[q, rng.integers(0, 16, N * K), at] = low[i]; tr[:, g] = y
            continue
        one = few[rng.integers(0, (1, 2, 4)[g % 3], (N, 1, G))]
        x = np.where(np.arange(16)[None, :, None] == rng.integers(0, 16, (N, 1, G)), one, x)
        tr[:, g] = np.where(rng.random((N, 1, G)) < (1.0 if g < 4 else 0.6), x, tr[:, g])
    return pack(tr, pa, s, ro)
def setup_inputs_block(rng):
    s, ro, w = batch(rng, [C - 1]); o = rng.permutation(8); f = int(o[4])
    if not np.any(s[f] == 0): s[f, int(rng.integers(0, N * K))] = 0
    for r in range(N):
        p = rng.permutation(G); v = (r - 1) % N
        ro[f, 0, r * K:(r + 1) * K] = r * G + p[:K]; ro[f, 1, v * K:(v + 1) * K] = r * G + p[K:2 * K]
    pa, live, dead = living(rng, s, ro, w, 0.05); tr = trunks(rng, s, ro, live, dead); sh = (N, 16, G); q = int(rng.integers(0, N))
    for h in range(5):
        g = int(o[h]); pa[g][:, C - 1] = ro[g][:, 0]
        top = np.union1d(live[g][live[g] >> SH == (C - 1) >> SH], np.array([C - 1])); d = np.setdiff1d(dead[g], np.array([C - 1]))
        full = top[rng.integers(0, len(top), sh)]; free = d[rng.integers(0, len(d), sh)]
        if h == 0: tr[:, g] = full
        if h == 1 or h == 2: tr[:, g] = free
        if h == 2: tr[q, g] = full[q]
        if h == 3: pa[g] = NONE
        if h == 4:
            a = np.arange(N * K) // K; b = (a + 1) % N; u = ro[g, 0] - a * G; v = ro[g, 1] - b * G; y = tr[:, g]
            y[a, rng.integers(0, 16, N * K), u] = d[rng.integers(0, len(d), N * K)]
            y[b, :, v] = full[b, :, v]; y[b[::4], rng.integers(0, 16, len(b[::4])), v[::4]] = s[g][::4]
    return pack(tr, pa, s, ro)
def setup_inputs_late(rng):
    s, ro, w = batch(rng); pa, live, dead = living(rng, s, ro, w, 0.05); tr = trunks(rng, s, ro, live, dead); sh = (N, 16, G)
    for g in range(8):
        tr[:, g] = np.where(rng.random(sh) < rng.choice(np.array([0.0, 0.5, 1.0]), (N, 1, G)), s[g][rng.integers(0, N * K, sh)], tr[:, g])
        u = np.argsort(s[g, :K])[:16]; v = K + np.argsort(s[g, K:2 * K])[-16:]
        y = tr[2, g]; y[:, ro[g, 1, v] - 2 * G] = s[g][u]
        for a, r, t in ((u, 0, 0), (v, 1, 0), (u, 0, 1)):
            y = tr[r + t, g]; y[:2, ro[g, t, a] - (r + t) * G] = dead[g][0]
        e = np.argsort(s[g, :K])[16:]; e = e[np.isin(ro[g, 1, e], ro[g, 0, K:2 * K], invert=True)]; lo, hi = e[:16], e[-16:]
        top = live[g][live[g] >> SH == (C - 1) >> SH]
        assert len(e) >= 32 and len(top) > 0 and np.all((s[g][lo] >> SH) < (s[g][hi] >> SH))
        assert np.all(np.any(pa[g][:, top] != NONE, axis=0)) and np.all(pa[g][:, dead[g][0]] == NONE)
        y = tr[0, g]; y[:2, ro[g, 0, np.append(lo, hi)]] = dead[g][0]
        y = tr[1, g]; y[:, ro[g, 1, lo] - G] = top[rng.integers(0, len(top), 16)]; y[:, ro[g, 1, hi] - G] = s[g][lo]
    return pack(tr, pa, s, ro)
def setup_inputs_spread(rng):
    s, ro, w = batch(rng); late = ro[:, RO:]; ro[:, RO:] = np.where(rng.random(late.shape) < 0.5, rng.integers(0, NONE, late.shape), late)
    pa, live, dead = living(rng, s, ro, w, 0.02); tr = trunks(rng, s, ro, live, dead)
    pa = np.where((pa != NONE) & (rng.random(pa.shape) < 0.5), np.minimum((NONE * rng.random(pa.shape) ** 4).astype(np.int64), NONE - 1), pa)
    x = np.minimum((C * rng.random(tr.shape) ** rng.choice(np.array([0.25, 1.0, 4.0]), (N, 8, 1, G))).astype(np.int64), C - 1)
    return pack(np.where(rng.random((N, 8, 1, G)) < 0.5, x, tr), pa, s, ro)
def check_inputs(d):
    bad = []
    for k, lo, hi in (("trunk", 0, C - 1), ("paths", 0, NONE), ("calls", 0, C - 1), ("routes", 0, NONE - 1)):
        if np.min(d[k]) < lo or np.max(d[k]) > hi: bad.append("range of " + k)
    if bad: return bad
    if np.any(d["paths"] != d["paths"][:1]): bad.append("paths alike on all ranks")
    s = np.concatenate([gentries(a) for a in d["calls"]], axis=1).astype(np.int64)
    if np.any(np.diff(np.sort(s, axis=1), axis=1) == 0): bad.append("calls of a group all different")
    if np.any(np.take_along_axis(d["paths"][0].reshape(8, 16, C), s[:, None, :], 2) != NONE): bad.append("paths of the seekers are none")
    own = (np.arange(N)[:, None] + np.arange(RO)[None, :]) % N
    at = d["routes"].astype(np.int64).reshape(N, 8, 16, K)[:, :, :RO] - own[:, None, :, None] * G
    if np.min(at) < 0 or np.max(at) > G - 1: bad.append("row t of routes names bundles of rank (r + t) mod N")
    if np.any(np.diff(np.sort(at, axis=3), axis=3) == 0): bad.append("row t of routes names different bundles")
    return bad
def reference(trunk, paths, calls, routes):
    tr = trunk.astype(np.int64).reshape(N, 8, 16, G); pa = paths[0].astype(np.int64).reshape(8, 16, C)
    sl = np.stack([gentries(a) for a in calls]).astype(np.int64); ro = routes.astype(np.int64).reshape(N, 8, 16, K)
    row = np.arange(16)[None, :, None]; D = C // N
    for t in range(RO):
        new = pa.copy(); gone = np.zeros((8, C), bool)
        for q in range(N):
            r = (q - t) % N; s = sl[r]; at = ro[r, :, t] - q * G
            hold = np.take_along_axis(tr[q], at[:, None, :], 2)
            hop = np.take_along_axis(pa, hold.reshape(8, 1, 16 * K), 2).reshape(8, 16, 16, K)
            dead = np.logical_not(np.any(hop != NONE, axis=1))
            like = np.add.reduce((hop == ro[r][:, :, None, :]).astype(np.int64), axis=1)
            may = (hold >> SH) < (s >> SH)[:, None, :]
            key = np.where(dead, 2 ** 22 + 15 - row, np.where(may, (like * C + C - 1 - hold) * 16 + 15 - row, -1))
            best = np.max(key, axis=1); p = 15 - (best & 15)
            go = np.any(np.take_along_axis(pa, s[:, None, :], 2) != NONE, axis=1) | (t == 0)
            won = go & (best >= 0); vic = np.take_along_axis(hold, p[:, None, :], 1)[:, 0]
            b, i = np.nonzero(won); tr[q, b, p[b, i], at[b, i]] = s[b, i]; new[b, t, s[b, i]] = ro[r, b, t, i]
            b, i = np.nonzero(won & (best < 2 ** 22)); gone[b, vic[b, i]] = True
            b, i = np.nonzero(go & (best < 0)); gone[b, s[b, i]] = True
        pa = np.where(gone[:, None, :], NONE, new)
    return {"yt": tr.reshape(N, 128, G).astype(np.float32), "yp": np.stack([pa[:, :, r * D:(r + 1) * D].reshape(128, D) for r in range(N)]).astype(np.float32)}

from concourse.bass import DstId, RemoteDMATransfer
from concourse.mybir import AluOpType as A, ActivationFunctionType as AF

N, G, C, K, RO = 4, 512, 2048, 256, 5
NONE = N * G
f32, b16, i32, u16 = "float32", "bfloat16", "int32", "uint16"
PR, PSK, PTF, PCF, PSL, PL, PW = 0, 256, 272, 288, 304, 320, 368
LK = 65536.0
OUT = 6400.0
PIECES = [(0, 0, 128, "s"), (1, 0, 64, "s"), (1, 64, 96, "s"), (1, 96, 128, "v")]
DORD = [0, 3, 1, 2]
LIKE = [(0, 0, 128, True, True), (1, 96, 128, True, False), (1, 0, 96, False, True)]
PRE = 2
WS = 5
FK = ["Fa", "Fb"]
FSK = ["FS%d" % t for t in range(RO)]


def sb(names, cols, dtype):
    return {n: ("sbuf", [128, cols], dtype) for n in names.split()}


SCRATCH = {
    **sb("iA", 1, i32), **sb("BP", 1, f32), **sb("MB", 2, f32), **sb("CC", 8, i32), **sb("CCf", 8, f32),
    **sb("iX", 144, f32), **sb("Z Z0", 144, b16), **sb("iG16 iG8 iWT Idf Idm BO IND", 128, f32), **sb("IREV Idb Idn BW Yf", 128, b16),
    **sb("i16t MK T1 HIF", 16, f32), **sb("CI TH BI HI LOI PPI T2", 16, i32), **sb("BL BD", 8, b16),
    **sb("iS SM0 Hf KH DIFF DM SC1 SD", 256, f32), **sb("iOF RI", 256, i32), **sb("OFFS H16", 256, u16),
    **sb("SMb ELIG Gs LOD SED LOS LOO SES SEO", 256, b16), **sb("iFI", 64, f32), **sb("OFI", 64, u16),
    **sb("LI", 80, i32), **sb("TI", 512, i32), **sb("XB XT", 32, f32), **sb("TR S0 YO", 512, f32), **sb("BS", 512, b16),
    **sb("F FS", 2048, i32), **sb("NI W OH", 2048, b16), **sb("E Gd", 4096, b16), **sb("RB0 RB1", 4096, f32),
    **sb("PK0 PK1 PK2 PK3", PW, f32), **sb("UL", 4 * 112, u16), **sb("KS", RO * N * 128, b16),
    **{n: ("psum", [128, 512], f32) for n in "pK pD pX pY pT pR pM".split()},
}
SEMAPHORES = (["cv", "cs", "ct", "cg", "lset"] + ["set%d" % r for r in range(N)] + ["kill%d" % t for t in range(RO)]
              + ["lk%d" % t for t in range(RO)] + ["d%d" % i for i in range(36)])


def rank_program(g, core, T, topo):
    q = T.rank_of(core)
    if q is None:
        return
    others = [(q + i) % N for i in (1, 2, 3)]

    def plan(a):
        chip = topo.cores_of(T.cores[a])
        away = [r for r in range(N) if T.cores[r] not in chip]
        near = [r for r in range(N) if r != a and T.cores[r] in chip]
        out = topo.engines(T.cores[a], T.cores[away[0]])
        res = {}
        for n, r in enumerate(away):
            k = len(out) // len(away)
            res[r] = out[n * k:(n + 1) * k]
        for n, r in enumerate(near):
            rest = [e for e in topo.engines(T.cores[a], T.cores[r]) if e not in out]
            k = len(rest) // len(near)
            res[r] = rest[n * k:(n + 1) * k]
        return res
    plans = [plan(r) for r in range(N)]

    queue = {"v": g.vector, "s": g.scalar, "t": g.tensor, "g": g, "y": g.sync}
    cnt, waited, lastw, readers, total, nd = {}, {}, {}, {}, {}, [0]

    def need(qn, toks):
        best = {}
        for s, v in toks:
            best[s] = max(best.get(s, 0), v)
        for s, v in sorted(best.items()):
            if waited.get((qn, s), 0) < v:
                queue[qn].wait_ge(T.sem[s], v)
                waited[(qn, s)] = v

    def hazards(qn, reads, writes):
        toks = []
        for k in reads + writes:
            ps = k[0] == "p"
            for (oq, s, v, far) in lastw.get(k, []):
                if not (ps and oq == qn):
                    toks.append((s, v))
            if ps or k in writes:
                for (oq, s, v, far) in readers.get(k, []):
                    if far or oq != qn:
                        toks.append((s, v))
        return toks

    def record(tok, reads, writes):
        for k in reads:
            if k not in writes:
                readers.setdefault(k, []).append(tok)
        for k in writes:
            lastw[k] = [tok]
            readers[k] = []

    def op(qn, fn, reads, writes):
        need(qn, hazards(qn, reads, writes))
        s = "c" + qn
        cnt[s] = cnt.get(s, 0) + 1
        fn().then_inc(T.sem[s], 1)
        total[s] = cnt[s]
        record((qn, s, cnt[s], False), reads, writes)

    def dma(qn, out_, in_, reads, writes):
        need(qn, hazards(qn, reads, writes))
        s = "d%d" % nd[0]
        nd[0] += 1
        queue[qn].dma_start(out_, in_).then_inc(T.sem[s], 16)
        total[s] = 16
        record((qn, s, 16, True), reads, writes)

    def arrive(key, s, v):
        lastw[key] = [("remote", s, v, True)]
        readers[key] = []
        total[s] = v

    def send(ap, reads, rsem, lsem):
        need("g", hazards("g", reads, []))
        tr = []
        for r in others:
            rid, pid = topo.addr(T.cores[r], core)
            tr.append(RemoteDMATransfer(dst_ids=[DstId(rid=rid, pnc=pid)], dma_engine_mask=sum(1 << e for e in plans[q][r]),
                                        remote_sem=T.sem[rsem], src=ap, dst=ap))
        g.remote_dma_fused(tr, local_sem=T.sem[lsem])
        total[lsem] = sum(len(plans[q][r]) for r in others)
        for k in reads:
            readers.setdefault(k, []).append(("g", lsem, total[lsem], True))

    V, S, E_ = g.vector, g.scalar, g.tensor

    def ts(o, i, s1, s2, a, b, reads, writes):
        if b is None:
            op("v", lambda: V.tensor_scalar(o, i, s1, None, a), reads, writes)
        else:
            op("v", lambda: V.tensor_scalar(o, i, s1, s2, a, b), reads, writes)

    def tt(o, i0, i1, a, reads, writes):
        op("v", lambda: V.tensor_tensor(o, i0, i1, a), reads, writes)

    def cp(o, i, reads, writes):
        op("v", lambda: V.tensor_copy(o, i), reads, writes)

    def fill(o, c, w):
        op("v", lambda: V.memset(o, c), [], [w])

    def act(o, i, reads, writes, func=AF.Copy, **kw):
        op("s", lambda: S.activation(o, i, func, **kw), reads, writes)

    def mm(o, l, r, st, sp, reads, writes):
        op("t", lambda: E_.matmul(o, l, r, st, sp), reads, writes)

    def scan(o, d0, d1, a, b, reads, writes):
        op("v", lambda: V.tensor_tensor_scan(o, d0, d1, 0.0, a, b), reads, writes)

    def iota(n, pat, base=0, cm=0, keys=None):
        o = T[n]
        if o.dtype == T.iA.dtype:
            op("g", lambda: g.iota(o[:], pat, base, cm), [], keys or [n])
        else:
            op("g", lambda: g.iota(o[:], pat, base, cm, allow_small_or_imprecise_dtypes=True), [], keys or [n])

    PKb = [T["PK%d" % r] for r in range(N)]
    own = PKb[q]
    pk = ["PK%d" % r for r in range(N)]
    ul = ["UL%d" % r for r in range(N)]
    for r in others:
        arrive(pk[r], "set%d" % r, len(plans[r][q]))

    def UL(r, a):
        return T.UL[:, 112 * r + a:112 * r + a + 16]

    def set_list(r):
        cp(T.UL[:, 112 * r:112 * r + 80], PKb[r][:, PCF:PW], [pk[r]] if r != q else ["OC", "OS", "OL1", "OL2", "OL3"], [ul[r]])

    rbuf = {0: "RB0", 1: "RB1", 2: "RB1", 3: "RB1", 4: "RB0"}

    def expand(t, *parts):
        r = (q - t) % N
        for i in parts:
            act(T[rbuf[t]][:, 1024 * i:1024 * i + 1024], PKb[r][:, PR:PR + 256].indirect(T.OFFS[:, 64 * i:64 * i + 64]),
                ["OR" if r == q else pk[r], "OFFS"], ["%s%d" % (rbuf[t], i)])

    def blist(t):
        if t == 0:
            return UL(q, 80), "ULa"
        if t == 4:
            return UL(q, 96), "ULb"
        r = (q - t) % N
        return UL(r, 16 + 16 * t), ul[r]

    def hold_v(t):
        L, lk = blist(t)
        cp(T.H16[:], T.TR[:].indirect(L), ["TR", lk], ["H16"])

    def hold_s(t):
        L, lk = blist(t)
        act(T.Hf[:], T.TR[:].indirect(L), ["TR", lk], ["Hf"])
        act(T.KH[:], T.TR[:].indirect(L), ["TR", lk, "BP"], ["KH"], func=AF.Identity, bias=T.BP[:], scale=-32.0)

    def hold_d(t):
        for h in range(2):
            mm(T.pR[:, 256 * h:256 * h + 256], T.Idm[:], T.Hf[:], False, h == 1, ["Idm", "Hf"], ["pR"])
        act(T.ELIG[:], T.pR[:, 256:512], ["pR", "MB1"], ["ELIG"], func=AF.Sign, bias=T.MB[:, 1:2])
        act(T.DIFF[:], T.pR[:, 0:256], ["pR"], ["DIFF"])

    def like(t, parts):
        for i in parts:
            b, j0, j1, first, last = LIKE[i]
            u, w = 2048 * b + 16 * j0, 2048 * b + 16 * j1
            tt(T.E[:, u:w], T.F[:].indirect(T.H16[:, 128 * b + j0:128 * b + j1]), T[rbuf[t]][:, u:w], A.is_equal,
               FK + ["H16"] + ["%s%d" % (rbuf[t], n) for n in range((128 * b + j0) // 64, (128 * b + j1 + 63) // 64)], ["E%d" % i])
            full = T.pK[:, 128 * b:128 * b + 128]
            if first:
                mm(full, T.KH[:, 128 * b:128 * b + 128], T.Idf[:], True, False, ["KH", "Idf"], ["pK"])
            for p in range(16):
                mm(T.pK[j0:j1, 128 * b + p:128 * b + 128:16], T.E[:, u + p:w:16], T.BL[:], False, False, ["E%d" % i, "BL"], ["pK"])
            if last:
                mm(full, T.ELIG[:, 128 * b:128 * b + 128], T.Idn[:], False, True, ["ELIG", "Idn"], ["pK"])

    WK = ["W%d" % l for l in range(16)]

    def build_w():
        for l in range(16):
            o, m = T.W[:, 128 * l:128 * l + 128], T.MK[:, 15 - l:16 - l]
            if l < WS:
                act(o, T.Yf[:], ["Yf", "MK"], [WK[l]], scale=m)
            else:
                ts(o, T.Yf[:], m, None, A.mult, None, ["Yf", "MK"], [WK[l]])

    def kills_t(t):
        mm(T.pY[:, 0:128], T.Idb[:], T.Yf[:], True, False, ["Idb", "Yf"], ["pY"])
        for n, r in enumerate([q] + others):
            c = ((t - 1) * N + r) * 128
            mm(T.pY[:, 0:128], T.KS[:, c:c + 128], T.Idb[:], False, n == N - 1, ["KS%d_%d" % (t - 1, r), "Idb"], ["pY"])

    def kills_v():
        ts(T.Yf[:], T.pY[:, 0:128], 1.0, None, A.min, None, ["pY"], ["Yf"])

    def dead_pass(t, qn):
        if t > 0 and qn == "v":
            r = (q - t) % N
            cp(T.Gs[:], T.W[:].indirect(UL(r, 16)), WK + [ul[r]], ["Gs"])
        for i, (b, j0, j1, e) in enumerate(PIECES):
            if e != qn:
                continue
            win = T.W[:].indirect(T.H16[:, 128 * b + j0:128 * b + j1])
            o = T.Gd[:, 2048 * b + 16 * j0:2048 * b + 16 * j1]
            if e == "s":
                act(o, win, WK + ["H16"], ["Gd%d" % i])
            else:
                cp(o, win, WK + ["H16"], ["Gd%d" % i])

    def dead_t(t):
        for i in DORD:
            b, j0, j1, e = PIECES[i]
            for p in range(16):
                o = T.pD[j0:j1, 128 * b + p:128 * b + 128:16]
                last = p == 15 and t > 0
                mm(o, T.Gd[:, 2048 * b + 16 * j0 + p:2048 * b + 16 * j1:16], T.BW[:, 8 * p:8 * p + 8], True, not last, ["Gd%d" % i, "BW"], ["pD"])
                if last:
                    mm(o, T.Gs[:, 128 * b + j0:128 * b + j1], T.BD[:], False, True, ["Gs", "BD"], ["pD"])

    def candidates(t):
        r = (q - t) % N
        scan(T.SC1[:], T.SM0[:], T.pK[:, 0:256], A.mult, A.max, ["SM0", "pK"], ["SC1"])
        tt(T.BI[:], T.SC1[:, 15::16], PKb[r][:, PSK:PSK + 16], A.max, ["SC1", pk[r]], ["BI"])
        ts(T.HI[:], T.BI[:], 5, 127, A.logical_shift_right, A.bitwise_and, ["BI"], ["HI"])
        ts(T.LOI[:], T.BI[:], 12, 15, A.logical_shift_right, A.bitwise_and, ["BI"], ["LOI"])
        ts(T.PPI[:], T.BI[:], 31, None, A.bitwise_and, None, ["BI"], ["PPI"])
        cp(T.HIF[:], T.HI[:], ["HI"], ["HIF"])
        for c in range(16):
            ts(T.OH[:, 128 * c:128 * c + 128], T.IREV[:], T.HIF[:, c:c + 1], None, A.is_equal, None, ["IREV", "HIF"], ["OH%d" % c])

    def decide(t):
        scan(T.SD[:], T.SM0[:], T.pD[:, 0:256], A.mult, A.max, ["SM0", "pD"], ["SD"])
        d = T.SD[:, 15::16]
        tt(T.LOD[:, 0::16], d, T.LOI[:], A.add, ["SD", "LOI"], ["LOD"])
        scan(T.LOS[:], T.SMb[:], T.LOD[:], A.mult, A.add, ["SMb", "LOD"], ["LOS"])
        ts(T.LOO[:], T.LOS[:], 0.0, None, A.is_equal, None, ["LOS"], ["LOO"])
        for gg in range(8):
            for b in range(2):
                c = 8 * b + gg
                mm(T.pX[:, 16 * gg:16 * gg + 16], T.OH[:, 128 * c:128 * c + 128], T.LOO[:, 16 * c:16 * c + 16], b == 0, b == 1, ["OH%d" % c, "LOO"], ["pX"])
        c = (t * N + q) * 128
        if t < 3:
            expand(t + 1, 0)
        act(T.KS[:, c:c + 128], T.pX[:, 0:128], ["pX"], ["KS%d_%d" % (t, q)])
        if t < 3:
            expand(t + 1, 1)
        send(T.KS[:, c:c + 128], ["KS%d_%d" % (t, q)], "kill%d" % t, "lk%d" % t)
        n = sum(len(plans[r][q]) for r in others)
        for r in others:
            arrive("KS%d_%d" % (t, r), "kill%d" % t, n)
        ts(T.T1[:], d, 0.0, None, A.is_equal, None, ["SD"], ["T1"])
        ts(T.T2[:], d, 1.0 / 64, None, A.mult, None, ["SD"], ["T2"])
        tt(T.T1[:], T.T1[:], T.PPI[:], A.mult, ["T1", "PPI"], ["T1"])
        tt(T.SED[:, 0::16], T.T1[:], T.T2[:], A.add, ["T1", "T2"], ["SED"])
        scan(T.SES[:], T.SMb[:], T.SED[:], A.mult, A.add, ["SMb", "SED"], ["SES"])
        ts(T.SEO[:], T.SES[:], 15.0, None, A.is_equal, None, ["SES"], ["SEO"])
        for b in range(2):
            mm(T.pT[:, 128 * b:128 * b + 128], T.SEO[:, 128 * b:128 * b + 128], T.Idb[:], True, True, ["SEO", "Idb"], ["pT"])
        tt(T.DM[:], T.pT[:, 0:256], T.DIFF[:], A.mult, ["pT", "DIFF"], ["DM"])
        L, lk = blist(t)
        tt(T.TR[:].indirect(L), T.Hf[:], T.DM[:], A.add, ["Hf", "DM", lk], ["TR"])

    dma("y", T.CI[:], T.calls[:], [], ["CI"])
    dma("s", T.RI[:], T.routes[:], [], ["RI"])
    dma("y", T.LI[:, 0:16], T.routes[0::16, :], [], ["LI0"])
    dma("s", T.TI[:], T.trunk[:], [], ["TI"])
    for h in range(2):
        dma("y", T.F[:, 1024 * h:1024 * h + 1024], T.paths[:, 1024 * h:1024 * h + 1024], [], [FK[h]])
    for t in range(1, RO):
        dma("s", T.LI[:, 16 * t:16 * t + 16], T.routes[t::16, :], [], ["LI%d" % t])
    iota("iOF", [[1, 16], [16, 16]])
    iota("iA", [[0, 1]], 0, 1)
    iota("iG16", [[1, 8], [0, 16]])
    iota("iX", [[1, 144]])
    iota("iG8", [[0, 16], [1, 8]])
    iota("i16t", [[1, 16]])
    iota("iS", [[0, 16], [1, 16]])
    iota("iWT", [[-64, 16], [0, 8]], 976)
    iota("iFI", [[16, 64]])
    iota("IREV", [[-1, 128]], 127)
    iota("FS", [[0, 2048]], 0, 0, FSK)
    fill(T.S0[:], 0.0, "S0")
    cp(T.OFFS[:], T.iOF[:], ["iOF"], ["OFFS"])
    ts(T.CC[:, 0:1], T.iA[:], 15, None, A.bitwise_and, None, ["iA"], ["CC0"])
    ts(T.CC[:, 1:2], T.iA[:], 4, None, A.logical_shift_right, None, ["iA"], ["CC1"])
    ts(T.CC[:, 2:3], T.iA[:], 4, 1, A.logical_shift_right, A.bitwise_and, ["iA"], ["CC2"])
    cp(T.CC[:, 3:4], T.iA[:], ["iA"], ["CC3"])
    ts(T.CC[:, 4:5], T.iA[:], 112, None, A.bitwise_and, None, ["iA"], ["CC4"])
    cp(T.CCf[:, 0:5], T.CC[:, 0:5], ["CC%d" % i for i in range(5)], ["CCf"])
    kc, gc, par, pc, g16 = [T.CCf[:, i:i + 1] for i in range(5)]
    ts(T.BP[:], kc, -1.0, -8 * LK + 2047 * 32 + 15, A.mult, A.add, ["CCf"], ["BP"])
    ts(T.BO[:], T.iG16[:], gc, None, A.is_equal, None, ["iG16", "CCf"], ["BO"])
    cp(own[:, PCF:PCF + 16], T.CI[:], ["CI"], ["OC"])
    ts(T.TH[:], T.CI[:], 3584, None, A.bitwise_and, None, ["CI"], ["TH"])
    cp(own[:, PTF:PTF + 16], T.TH[:], ["TH"], ["OT"])

    def load_s0(r):
        dma("y", T.S0[0::16, 0:256], PKb[r][:, PCF:PCF + 16], ["OC" if r == q else pk[r]], ["S0"])
        dma("y", T.S0[0::16, 256:512], PKb[r][:, PTF:PTF + 16], ["OT" if r == q else pk[r]], ["S0"])

    def load_sr():
        mm(T.pR[:, 0:512], T.BO[:], T.S0[:], True, False, ["BO", "S0"], ["pR"])

    def none_s(tab, keys):
        act(T.NI[:, 1024:2048], tab[:, 1024:2048].indirect(T.OFI[:]), keys + ["OFI", "MB"], ["NI1"], func=AF.Relu, bias=T.MB[:, 0:1])

    def none_v(tab, keys):
        ts(T.NI[:, 0:1024], tab[:, 0:1024], float(NONE), None, A.is_equal, None, keys, ["NI0"])

    load_s0(q)
    for t in range(RO):
        dma("y", T.FS[t::16, :], T.paths[t::16, :], [], ["FS%d" % t])
    cp(own[:, PR:PR + 256], T.RI[:], ["RI"], ["OR"])
    expand(0, 0, 1)
    ts(UL(q, 80), T.LI[:, 0:16], -q * G, None, A.add, None, ["LI0"], ["ULa"])
    cp(T.TR[:], T.TI[:], ["TI"], ["TR"])
    hold_v(0)
    hold_s(0)
    expand(0, 3)
    ts(T.IND[:], T.iG8[:], gc, None, A.is_equal, None, ["iG8", "CCf"], ["IND"])
    ts(T.XB[:, 16:32], T.CI[:], par, None, A.mult, None, ["CI", "CCf"], ["XBo"])
    tt(T.XB[:, 0:16], own[:, PCF:PCF + 16], T.XB[:, 16:32], A.subtract, ["OC", "XBo"], ["XBe"])
    op("v", lambda: V.transpose(T.XT[:], T.XB[:]), ["XBo", "XBe"], ["XT"])
    for t in (1, 2, 3):
        ts(own[:, PL + 16 * t - 16:PL + 16 * t], T.LI[:, 16 * t:16 * t + 16], -((q + t) % N * G), None, A.add, None, ["LI%d" % t], ["OL%d" % t])
    tt(own[:, PSL:PSL + 16], T.XT[:, 0:16], T.XT[:, 16:32], A.add, ["XT"], ["OS"])
    for b in range(2):
        mm(T.pM[:, 8 * b:8 * b + 8], T.S0[:, 128 * b:128 * b + 128], T.IND[:, 0:8], True, True, ["S0", "IND"], ["pM"])
    load_sr()
    ts(T.Idf[:], T.iX[:, 0:128], pc, None, A.is_equal, None, ["iX", "CCf"], ["Idf"])
    ts(T.Idb[:], T.iX[:, 0:128], pc, None, A.is_equal, None, ["iX", "CCf"], ["Idb"])
    ts(T.Idm[:], T.Idf[:], -1.0, None, A.mult, None, ["Idf"], ["Idm"])
    fill(T.MB[:, 1:2], -0.5, "MB1")
    ts(own[:, PSK:PSK + 16], T.pM[:, 0:16], -32.0, 2047.0 * 32 + 16, A.mult, A.add, ["pM"], [pk[q]])
    send(own[:], [pk[q], "OC", "OT", "OR", "OS", "OL1", "OL2", "OL3"], "set%d" % q, "lset")
    ts(T.CCf[:, 5:6], g16, 15.0, None, A.add, None, ["CCf"], ["CCf5"])
    ts(T.Z[:], T.iX[:], T.CCf[:, 5:6], None, A.is_equal, None, ["iX", "CCf5"], ["Z"])
    ts(T.MK[:], T.i16t[:], kc, None, A.is_equal, None, ["i16t", "CCf"], ["MK"])
    ts(T.Idn[:], T.Idb[:], 9.0 * LK, None, A.mult, None, ["Idb"], ["Idn"])
    tt(T.BW[:], T.IND[:], T.iWT[:], A.mult, ["IND", "iWT"], ["BW"])
    ts(T.BL[:], T.IND[:, 0:8], LK, None, A.mult, None, ["IND"], ["BL"])
    ts(T.BD[:], T.IND[:, 0:8], OUT, None, A.mult, None, ["IND"], ["BD"])
    ts(T.SM0[:], T.iS[:], 1.0, None, A.min, None, ["iS"], ["SM0"])
    ts(T.SMb[:], T.iS[:], 1.0, None, A.min, None, ["iS"], ["SMb"])
    fill(T.LOD[:], -1.0, "LOD")
    fill(T.SED[:], 1.0, "SED")
    fill(T.MB[:, 0:1], -2047.0, "MB")
    ts(T.OFI[:], T.iFI[:], kc, None, A.add, None, ["iFI", "CCf"], ["OFI"])
    none_s(T.F, ["Fb"])
    hold_d(0)
    expand(0, 2)
    ts(UL(q, 96), T.LI[:, 64:80], -q * G, None, A.add, None, ["LI4"], ["ULb"])
    set_list(q)
    ts(T.Z0[:], T.Z[:], T.MK[:, 0:1], None, A.mult, None, ["Z", "MK"], ["Z0"])

    none_v(T.F, ["Fa"])
    for l in range(16):
        mm(T.pY[:, 0:128], T.Z[:, l:l + 128], T.NI[:, 128 * l:128 * l + 128], l == 0, l == 15, ["Z", "NI%d" % (l // 8)], ["pY"])
    like(0, range(PRE))
    ts(T.Yf[:], T.pY[:, 0:128], 16.0, None, A.is_ge, None, ["pY"], ["Yf"])
    build_w()
    dead_pass(0, "s")
    like(0, range(PRE, 3))
    dead_pass(0, "v")
    for t in range(RO):
        if t < 4:
            load_s0((q - t - 1) % N)
        dead_t(t)
        candidates(t)
        if t > 0:
            dma("y", T.F[t::16, :], T.FS[t::16, :], ["FS%d" % t], FK)
        decide(t)
        if t == 4:
            break
        load_sr()
        if t == 0:
            set_list(others[2])
        hold_v(t + 1)
        hold_s(t + 1)
        if t < 3:
            expand(t + 1, 3)
        hold_d(t + 1)
        if t < 3:
            expand(t + 1, 2)
        if t == 0:
            cp(T.FS[:].indirect(UL(q, 0)), own[:, PR:PR + 256], [ul[q], "OR"], FSK)
            for r in [others[2], others[1], others[0]]:
                if r != others[2]:
                    set_list(r)
                cp(T.FS[:].indirect(UL(r, 0)), PKb[r][:, PR:PR + 256], [ul[r], pk[r]], FSK)
            dma("y", T.F[0::16, :], T.FS[0::16, :], ["FS0"], FK)
            none_s(T.FS, FSK)
            none_v(T.FS, FSK)
            mm(T.pY[:, 0:128], T.Idb[:], T.Yf[:], True, False, ["Idb", "Yf"], ["pY"])
            for l in range(16):
                mm(T.pY[:, 0:128], T.Z0[:, l:l + 128], T.NI[:, 128 * l:128 * l + 128], False, l == 15, ["Z0", "NI%d" % (l // 8)], ["pY"])
            ts(T.Yf[:], T.pY[:, 0:128], 2.0, None, A.is_ge, None, ["pY"], ["Yf"])
            kills_t(1)
        else:
            kills_t(t + 1)
            like(t + 1, range(PRE))
        kills_v()
        build_w()
        dead_pass(t + 1, "s")
        like(t + 1, range(3) if t == 0 else range(PRE, 3))
        dead_pass(t + 1, "v")
    dma("y", T.yt[:], T.TR[:], ["TR"], ["yt"])
    for l in range(4):
        m = 15 - 4 * q - l
        ts(T.BS[:, 128 * l:128 * l + 128], T.BO[:], T.MK[:, m:m + 1], float(NONE), A.mult, A.mult, ["BO", "MK"], ["BS"])
    kills_t(RO)
    kills_v()
    for l in range(4):
        mm(T.pM[:, 128 * l:128 * l + 128], T.BS[:, 128 * l:128 * l + 128], T.Yf[:], True, True, ["BS", "Yf"], ["pM"])
    tt(T.YO[:], T.pM[:, 0:512], T.F[:, G * q:G * q + G], A.max, ["pM"] + FK, ["YO"])
    dma("y", T.yp[:], T.YO[:], ["YO"], ["yp"])
    need("g", [(s, v) for s, v in total.items()])
